import numpy as np
import ml_dtypes


def mxq(x, axis, fmt="e4m3"):
    dtype, down = {"e4m3": (ml_dtypes.float8_e4m3fn, 7), "e5m2": (ml_dtypes.float8_e5m2, 14)}[fmt]
    v = np.moveaxis(np.asarray(x, np.float32).astype(ml_dtypes.bfloat16).astype(np.float64), axis, -1)
    blocks = v.reshape(v.shape[:-1] + (-1, 32))
    amax = np.abs(blocks).max(-1, keepdims=True)
    byte = np.maximum(np.where(amax > 0, np.frexp(amax)[1] - 1 + 127, 0) - down, 1)
    scale = np.exp2(byte - 127.0)
    codes = (blocks / scale).astype(np.float32).astype(dtype).astype(np.float64)
    return np.moveaxis((codes * scale).reshape(v.shape), -1, axis)


WIDE = False


def mx_kscale(k):
    if not WIDE:
        return np.ones(k)
    levels = np.array([30, -30])
    if k % 512:
        return np.exp2(np.random.permutation(np.resize(levels, k // 32))).repeat(32)
    a = np.empty((k // 512, 16))
    for p in range(k // 512):
        a[p, :8] = np.random.permutation(np.resize(levels, 8))
        for g in range(8):
            far = levels[np.abs(levels - a[p, g]) >= 10]
            a[p, g + 8] = far[np.random.randint(len(far))]
    return np.exp2(a.ravel()).repeat(32)


def f64(x):
    return np.asarray(x).astype(np.float64)


def striped(idx):
    return np.tile(np.asarray(idx).reshape(-1, 16).T, (8, 1)).astype(np.uint16)


def unstriped(offs):
    return offs[:16].T.reshape(-1).astype(np.int64)


E2M1 = np.array([0.0, 0.5, 1.0, 1.5, 2.0, 3.0, 4.0, 6.0, -0.0, -0.5, -1.0, -1.5, -2.0, -3.0, -4.0, -6.0])


def pack_weight(w, fmt):
    k, n = w.shape
    w = f64(np.asarray(w, np.float32).astype(ml_dtypes.bfloat16)).reshape(k // 32, 32, n)
    amax = np.abs(w).max(1)
    if fmt in ("e4m3", "e5m2"):
        byte = np.frexp(amax)[1] - 1 + 127 - (7 if fmt == "e4m3" else 14)
    else:
        mant, ex = np.frexp(amax / 6.0)
        byte = np.where(mant > 0.5, ex, ex - 1) + 127
    byte = np.clip(np.where(amax > 0, byte, 1), 1, 254)
    scaled = (w * np.exp2(127.0 - byte)[:, None, :]).reshape(k, n).astype(np.float32)
    by_word = np.ascontiguousarray(scaled.reshape(k // 512, 128, 4, n).transpose(0, 1, 3, 2))
    if fmt in ("e4m3", "e5m2"):
        words = by_word.astype(ml_dtypes.float8_e4m3fn if fmt == "e4m3" else ml_dtypes.float8_e5m2).view(np.uint8)
    else:
        c = by_word.astype(ml_dtypes.float4_e2m1fn).view(np.uint8) & 0xF
        words = (c[..., 0::2] | (c[..., 1::2] << 4)).reshape(k // 512, 128, 2 * n)
    return np.ascontiguousarray(words), np.ascontiguousarray(byte.astype(np.uint8).reshape(k // 512, 16, n))


def unpack_weight(words, scales, fmt):
    g, _, n = scales.shape
    words = np.ascontiguousarray(words).reshape(g, 128, n, -1)
    if fmt in ("e4m3", "e5m2"):
        vals = words.view(ml_dtypes.float8_e4m3fn if fmt == "e4m3" else ml_dtypes.float8_e5m2).astype(np.float64)
    else:
        nib = np.empty((g, 128, n, 4), np.uint8)
        nib[..., 0::2] = words & 0xF
        nib[..., 1::2] = words >> 4
        vals = E2M1[nib]
    vals = vals * np.repeat(np.exp2(scales.astype(np.float64) - 127.0), 8, axis=1)[..., None]
    return vals.transpose(0, 1, 3, 2).reshape(g * 512, n)


K, T, J, N, L = 1024, 1024, 256, 256, 512


def setup_inputs():
    n = np.random.standard_normal
    idx = np.random.permutation(T)[:J]
    fk = mx_kscale(K)
    fl = mx_kscale(L)
    xtp = pack_weight(n((K, T)) * np.random.uniform(0.4, 1.6, (1, T)) / fk[:, None], "e5m2")
    wap = pack_weight(n((K, N)) * 1 / np.sqrt(K) * fk[:, None], "e2m1")
    wbp = pack_weight(n((L, N)) * 1 / np.sqrt(L) * fl[:, None], "e2m1")
    return {
        "xt_words": xtp[0],
        "xt_scales": xtp[1],
        "wa_words": wap[0],
        "wa_scales": wap[1],
        "sx": (n((L, J)) * np.random.uniform(0.4, 1.6, (1, J)) / fl[:, None]).astype(np.float32),
        "wb_words": wbp[0],
        "wb_scales": wbp[1],
        "bi": (np.random.uniform(-0.6, 0.6, (1, N))).astype(np.float32),
        "gm": (np.random.uniform(0.5, 2.0, (1, N))).astype(np.float32),
        "offs": striped(idx),
    }


def reference(xt_words, xt_scales, wa_words, wa_scales, sx, wb_words, wb_scales, bi, gm, offs):
    idx = unstriped(offs)
    xtu = unpack_weight(xt_words, xt_scales, "e5m2")
    wau = unpack_weight(wa_words, wa_scales, "e2m1")
    wbu = unpack_weight(wb_words, wb_scales, "e2m1")
    xtidxg = xtu[:, idx]
    a = xtidxg.T @ wau
    sxq = mxq(f64(sx), 0, "e5m2")
    b0 = sxq.T @ wbu
    b2 = b0 + f64(bi)
    d1 = np.mean(np.square(a - b2), axis=1, keepdims=True)
    y = a * f64(gm) / (0.4 + d1)
    return y

@@ -1,0 +1,163 @@
+import math
+from contextlib import ExitStack
+
+import concourse.mybir as mybir
+from concourse.masks import make_identity
+
+K, T, J, N, L = 1024, 1024, 256, 256, 512
+FLOPS = 2 * J * N * (K + L)
+
+F32 = mybir.dt.float32
+BF16 = mybir.dt.bfloat16
+I32 = mybir.dt.int32
+U32 = mybir.dt.uint32
+U16 = mybir.dt.uint16
+U8 = mybir.dt.uint8
+E5M2X4 = mybir.dt.float8_e5m2_x4
+E2M1X4 = mybir.dt.float4_e2m1fn_x4
+ALU = mybir.AluOpType
+ACT = mybir.ActivationFunctionType
+
+P = 128
+PACK = 4
+PASSES = K // (P * PACK)
+TILES = J // P
+LANES = 4
+EPS = 0.4
+
+
+def load_scale_rows(engine, plane, scales, lanes=range(LANES)):
+    rows = scales.rearrange("z (q r) c -> r q z c", r=LANES)
+    for r in lanes:
+        engine.dma_start(out=plane[r:P:32, :, :], in_=rows[r].bitcast(I32))
+
+
+def tile_list_rows_owninput_bygapsize_kernel(
+    tc, xt_words, xt_scales, wa_words, wa_scales, sx, wb_words, wb_scales, bi, gm, offs, out
+):
+    nc = tc.nc
+    with ExitStack() as ctx:
+        keep = ctx.enter_context(tc.tile_pool(name="keep", bufs=1))
+        psum = ctx.enter_context(tc.psum_pool(name="psum", bufs=1))
+
+        offsets = keep.tile([P, J // 16], U16, name="offsets")
+        xs_table = keep.tile([P, PASSES, T // 4], I32, name="xs_table", align_bytes=64)
+        wa_plane = keep.tile([P, PASSES, N // 4], I32, name="wa_plane", align_bytes=64)
+        wb_plane = keep.tile([P, 1, N // 4], I32, name="wb_plane", align_bytes=64)
+        ident = keep.tile([P, P], F32, name="ident")
+        ones = keep.tile([P, TILES, 1], F32, name="ones")
+        gap = keep.tile([P, TILES, N + 8], F32, name="gap")
+
+        nc.vector.memset(xs_table[:, 0, :], 0)
+        nc.gpsimd.memset(xs_table[:, 1, :], 0)
+        nc.vector.memset(ident[:], 0.0)
+        nc.vector.memset(ones[:], 1.0)
+        make_identity(nc, ident[:], nomemset=True)
+        nc.scalar.activation(out=gap[:, :, N : N + 1], in_=ones[:], func=ACT.Copy, scale=math.sqrt(EPS * N))
+
+        xw_table = [keep.tile([P, T], I32, name="xw_table%d" % z, align_bytes=64) for z in range(PASSES)]
+        sx_raw = keep.tile([P, PACK, J], F32, name="sx_raw")
+        wa_codes = keep.tile([P, PASSES, N // 2], I32, name="wa_codes", align_bytes=64)
+        wb_codes = keep.tile([P, N // 2], I32, name="wb_codes", align_bytes=64)
+        bi_cols = keep.tile([P, 2], F32, name="bi_cols")
+        gm_cols = keep.tile([P, 2], F32, name="gm_cols")
+
+        def load_words(z):
+            nc.sync.dma_start(out=xw_table[z][:], in_=xt_words[z].rearrange("p c r -> p (c r)").bitcast(I32))
+
+        nc.sync.dma_start(offsets[:], offs)
+        nc.sync.dma_start(out=bi_cols[:], in_=bi.rearrange("o (p c) -> (o p) c", c=2))
+        load_scale_rows(nc.sync, xs_table, xt_scales)
+        nc.sync.dma_start(out=sx_raw[:], in_=sx.rearrange("(p t) j -> p t j", t=PACK))
+        load_words(0)
+        load_scale_rows(nc.sync, wb_plane, wb_scales)
+        nc.sync.dma_start(out=wb_codes[:], in_=wb_words[0].bitcast(I32))
+        nc.sync.dma_start(out=gm_cols[:], in_=gm.rearrange("o (p c) -> (o p) c", c=2))
+        load_words(1)
+        nc.sync.dma_start(out=wa_codes[:], in_=wa_words.rearrange("z p c -> p z c").bitcast(I32))
+        load_scale_rows(nc.gpsimd, wa_plane, wa_scales)
+
+        def spread(cols, name):
+            bank = psum.tile([P, 2, P], F32, name=name + "_bank")
+            for c in range(2):
+                nc.tensor.transpose(bank[:, c, :], cols[:, c : c + 1].to_broadcast([P, P]), ident[:])
+            rows = keep.tile([P, P, 2], F32, name=name + "_rows")
+            nc.scalar.copy(out=rows[:], in_=bank[:].rearrange("p c i -> p i c"))
+            return rows[:].rearrange("p i c -> p (i c)")
+
+        bi_rows = spread(bi_cols, "bi")
+
+        xs_picked = keep.tile([P, PASSES, J], U8, name="xs_picked", align_bytes=64)
+        for z in range(PASSES):
+            nc.vector.tensor_copy(out=xs_picked[:, z, :], in_=xs_table[:, z, :].bitcast(U8).indirect(offsets[:]))
+
+        sx_codes = keep.tile([P, J], U32, name="sx_codes", align_bytes=64)
+        sx_plane = keep.tile([P, J], U8, name="sx_plane", align_bytes=64)
+        b0 = psum.tile([P, TILES, N], F32, name="b0")
+        for t in range(TILES):
+            cols = slice(t * P, (t + 1) * P)
+            grouped = keep.tile([P, P, PACK], BF16, name="sx_grouped%d" % t, align_bytes=64)
+            nc.scalar.copy(
+                out=grouped[:].rearrange("p (c i) r -> p c r i", i=4),
+                in_=sx_raw[:, :, cols].rearrange("p r (c i) -> p c r i", i=4),
+            )
+            nc.vector.quantize_mx(
+                out=sx_codes[:, cols].bitcast(E5M2X4),
+                scales=sx_plane[:, cols],
+                in_=grouped[:].rearrange("p c r -> p (c r)"),
+            )
+            nc.tensor.matmul_mx(
+                out=b0[:, t, :],
+                lhsT=sx_codes[:, cols].bitcast(E5M2X4),
+                lhsT_scale=sx_plane[:, cols],
+                rhs=wb_codes[:].bitcast(U8).bitcast(E2M1X4),
+                rhs_scale=wb_plane[:, 0, :].bitcast(U8),
+                start=True,
+                stop=True,
+            )
+
+        xw_picked = keep.tile([P, PASSES, J], U32, name="xw_picked", align_bytes=64)
+        a = [psum.tile([P, N], F32, name="a%d" % t) for t in range(TILES)]
+
+        def a_pass(z, t):
+            cols = slice(t * P, (t + 1) * P)
+            nc.tensor.matmul_mx(
+                out=a[t][:],
+                lhsT=xw_picked[:, z, cols].bitcast(E5M2X4),
+                lhsT_scale=xs_picked[:, z, cols],
+                rhs=wa_codes[:, z, :].bitcast(U8).bitcast(E2M1X4),
+                rhs_scale=wa_plane[:, z, :].bitcast(U8),
+                start=(z == 0),
+                stop=(z == PASSES - 1),
+            )
+
+        nc.vector.tensor_copy(out=xw_picked[:, 0, :], in_=xw_table[0][:].bitcast(U32).indirect(offsets[:]))
+        b2 = keep.tile([P, TILES, N], F32, name="b2")
+        nc.vector.tensor_tensor(
+            out=b2[:], in0=b0[:], in1=bi_rows.unsqueeze(1).to_broadcast([P, TILES, N]), op=ALU.add
+        )
+        gm_rows = spread(gm_cols, "gm")
+        for t in range(TILES):
+            a_pass(0, t)
+        for t in range(TILES):
+            nc.vector.tensor_copy(
+                out=xw_picked[:, 1, t * P : (t + 1) * P],
+                in_=xw_table[1][:].bitcast(U32).indirect(offsets[:, t * (P // 16) : (t + 1) * (P // 16)]),
+            )
+            a_pass(1, t)
+
+        squares = keep.tile([P, TILES, N + 1], F32, name="squares")
+        for t in range(TILES):
+            nc.vector.tensor_tensor(out=gap[:, t, 0:N], in0=a[t][:], in1=b2[:, t, :], op=ALU.subtract)
+        for t in range(TILES):
+            denom = keep.tile([P, 1], F32, name="denom%d" % t)
+            inverse = keep.tile([P, 1], F32, name="inverse%d" % t)
+            result = keep.tile([P, N], F32, name="result%d" % t)
+            nc.scalar.activation(
+                out=squares[:, t, :], in_=gap[:, t, 0 : N + 1], func=ACT.Square, scale=1.0 / math.sqrt(N), accum_out=denom[:]
+            )
+            nc.vector.reciprocal(out=inverse[:], in_=denom[:])
+            nc.vector.scalar_tensor_tensor(
+                out=result[:], in0=a[t][:], scalar=inverse[:], in1=gm_rows, op0=ALU.mult, op1=ALU.mult
+            )
+            (nc.sync if t == 0 else nc.scalar).dma_start(out=out[t * P : (t + 1) * P, :], in_=result[:])

@@ -67,15 +67,17 @@ def tile_list_rows_owninput_bygapsize_kernel(
 
         nc.sync.dma_start(offsets[:], offs)
         nc.sync.dma_start(out=bi_cols[:], in_=bi.rearrange("o (p c) -> (o p) c", c=2))
+        load_scale_rows(nc.sync, wa_plane, wa_scales, [2])
         load_scale_rows(nc.sync, xs_table, xt_scales)
         nc.sync.dma_start(out=sx_raw[:], in_=sx.rearrange("(p t) j -> p t j", t=PACK))
+        nc.sync.dma_start(out=wb_codes[:], in_=wb_words[0].bitcast(I32))
         load_words(0)
         load_scale_rows(nc.sync, wb_plane, wb_scales)
-        nc.sync.dma_start(out=wb_codes[:], in_=wb_words[0].bitcast(I32))
-        nc.sync.dma_start(out=gm_cols[:], in_=gm.rearrange("o (p c) -> (o p) c", c=2))
         load_words(1)
         nc.sync.dma_start(out=wa_codes[:], in_=wa_words.rearrange("z p c -> p z c").bitcast(I32))
-        load_scale_rows(nc.gpsimd, wa_plane, wa_scales)
+        load_scale_rows(nc.sync, wa_plane, wa_scales, [3])
+        nc.sync.dma_start(out=gm_cols[:], in_=gm.rearrange("o (p c) -> (o p) c", c=2))
+        load_scale_rows(nc.gpsimd, wa_plane, wa_scales, [0, 1])
 
         def spread(cols, name):
             bank = psum.tile([P, 2, P], F32, name=name + "_bank")
@@ -93,7 +95,7 @@ def tile_list_rows_owninput_bygapsize_kernel(
 
         sx_codes = keep.tile([P, J], U32, name="sx_codes", align_bytes=64)
         sx_plane = keep.tile([P, J], U8, name="sx_plane", align_bytes=64)
-        b0 = psum.tile([P, TILES, N], F32, name="b0")
+        b0 = [psum.tile([P, N], F32, name="b0_%d" % t) for t in range(TILES)]
         for t in range(TILES):
             cols = slice(t * P, (t + 1) * P)
             grouped = keep.tile([P, P, PACK], BF16, name="sx_grouped%d" % t, align_bytes=64)
@@ -107,7 +109,7 @@ def tile_list_rows_owninput_bygapsize_kernel(
                 in_=grouped[:].rearrange("p c r -> p (c r)"),
             )
             nc.tensor.matmul_mx(
-                out=b0[:, t, :],
+                out=b0[t][:],
                 lhsT=sx_codes[:, cols].bitcast(E5M2X4),
                 lhsT_scale=sx_plane[:, cols],
                 rhs=wb_codes[:].bitcast(U8).bitcast(E2M1X4),
@@ -133,9 +135,8 @@ def tile_list_rows_owninput_bygapsize_kernel(
 
         nc.vector.tensor_copy(out=xw_picked[:, 0, :], in_=xw_table[0][:].bitcast(U32).indirect(offsets[:]))
         b2 = keep.tile([P, TILES, N], F32, name="b2")
-        nc.vector.tensor_tensor(
-            out=b2[:], in0=b0[:], in1=bi_rows.unsqueeze(1).to_broadcast([P, TILES, N]), op=ALU.add
-        )
+        for t in range(TILES):
+            nc.vector.tensor_tensor(out=b2[:, t, :], in0=b0[t][:], in1=bi_rows, op=ALU.add)
         gm_rows = spread(gm_cols, "gm")
         for t in range(TILES):
             a_pass(0, t)
@@ -147,17 +148,19 @@ def tile_list_rows_owninput_bygapsize_kernel(
             a_pass(1, t)
 
         squares = keep.tile([P, TILES, N + 1], F32, name="squares")
+        scaled = keep.tile([P, TILES, N], F32, name="scaled")
+        denom = [keep.tile([P, 1], F32, name="denom%d" % t) for t in range(TILES)]
+        inverse = [keep.tile([P, 1], F32, name="inverse%d" % t) for t in range(TILES)]
+        result = [keep.tile([P, N], F32, name="result%d" % t) for t in range(TILES)]
         for t in range(TILES):
             nc.vector.tensor_tensor(out=gap[:, t, 0:N], in0=a[t][:], in1=b2[:, t, :], op=ALU.subtract)
-        for t in range(TILES):
-            denom = keep.tile([P, 1], F32, name="denom%d" % t)
-            inverse = keep.tile([P, 1], F32, name="inverse%d" % t)
-            result = keep.tile([P, N], F32, name="result%d" % t)
             nc.scalar.activation(
-                out=squares[:, t, :], in_=gap[:, t, 0 : N + 1], func=ACT.Square, scale=1.0 / math.sqrt(N), accum_out=denom[:]
+                out=squares[:, t, :], in_=gap[:, t, 0 : N + 1], func=ACT.Square, scale=1.0 / math.sqrt(N), accum_out=denom[t][:]
             )
-            nc.vector.reciprocal(out=inverse[:], in_=denom[:])
-            nc.vector.scalar_tensor_tensor(
-                out=result[:], in0=a[t][:], scalar=inverse[:], in1=gm_rows, op0=ALU.mult, op1=ALU.mult
-            )
-            (nc.sync if t == 0 else nc.scalar).dma_start(out=out[t * P : (t + 1) * P, :], in_=result[:])
+        for t in range(TILES):
+            nc.vector.tensor_tensor(out=scaled[:, t, :], in0=a[t][:], in1=gm_rows, op=ALU.mult)
+            nc.vector.reciprocal(out=inverse[t][:], in_=denom[t][:])
+        nc.scalar.activation(out=result[0][:], in_=scaled[:, 0, :], func=ACT.Copy, scale=inverse[0][:])
+        nc.scalar.dma_start(out=out[0:P, :], in_=result[0][:])
+        nc.vector.tensor_scalar(out=result[1][:], in0=scaled[:, 1, :], scalar1=inverse[1][:], scalar2=None, op0=ALU.mult)
+        nc.sync.dma_start(out=out[P : 2 * P, :], in_=result[1][:])

@@ -65,19 +65,17 @@ def tile_list_rows_owninput_bygapsize_kernel(
         def load_words(z):
             nc.sync.dma_start(out=xw_table[z][:], in_=xt_words[z].rearrange("p c r -> p (c r)").bitcast(I32))
 
-        nc.sync.dma_start(offsets[:], offs)
-        nc.sync.dma_start(out=bi_cols[:], in_=bi.rearrange("o (p c) -> (o p) c", c=2))
-        load_scale_rows(nc.sync, wa_plane, wa_scales, [2])
-        load_scale_rows(nc.sync, xs_table, xt_scales)
         nc.sync.dma_start(out=sx_raw[:], in_=sx.rearrange("(p t) j -> p t j", t=PACK))
-        nc.sync.dma_start(out=wb_codes[:], in_=wb_words[0].bitcast(I32))
+        nc.sync.dma_start(offsets[:], offs)
+        load_scale_rows(nc.sync, xs_table, xt_scales)
+        nc.sync.dma_start(out=bi_cols[:], in_=bi.rearrange("o (p c) -> (o p) c", c=2))
         load_words(0)
+        nc.sync.dma_start(out=gm_cols[:], in_=gm.rearrange("o (p c) -> (o p) c", c=2))
+        nc.sync.dma_start(out=wb_codes[:], in_=wb_words[0].bitcast(I32))
         load_scale_rows(nc.sync, wb_plane, wb_scales)
         load_words(1)
         nc.sync.dma_start(out=wa_codes[:], in_=wa_words.rearrange("z p c -> p z c").bitcast(I32))
-        load_scale_rows(nc.sync, wa_plane, wa_scales, [3])
-        nc.sync.dma_start(out=gm_cols[:], in_=gm.rearrange("o (p c) -> (o p) c", c=2))
-        load_scale_rows(nc.gpsimd, wa_plane, wa_scales, [0, 1])
+        load_scale_rows(nc.sync, wa_plane, wa_scales)
 
         def spread(cols, name):
             bank = psum.tile([P, 2, P], F32, name=name + "_bank")
@@ -139,13 +137,12 @@ def tile_list_rows_owninput_bygapsize_kernel(
             nc.vector.tensor_tensor(out=b2[:, t, :], in0=b0[t][:], in1=bi_rows, op=ALU.add)
         gm_rows = spread(gm_cols, "gm")
         for t in range(TILES):
-            a_pass(0, t)
-        for t in range(TILES):
             nc.vector.tensor_copy(
                 out=xw_picked[:, 1, t * P : (t + 1) * P],
                 in_=xw_table[1][:].bitcast(U32).indirect(offsets[:, t * (P // 16) : (t + 1) * (P // 16)]),
             )
-            a_pass(1, t)
+            for z in range(PASSES):
+                a_pass(z, t)
 
         squares = keep.tile([P, TILES, N + 1], F32, name="squares")
         scaled = keep.tile([P, TILES, N], F32, name="scaled")

@@ -22,14 +22,19 @@ P = 128
 PACK = 4
 PASSES = K // (P * PACK)
 TILES = J // P
-LANES = 4
+QUADRANT = 32
+SCALE_ROWS = 4
+LIST_ROWS = 16
+LINE = 4
+PAIR = N // P
+ROW_PAD = 8
 EPS = 0.4
 
 
-def load_scale_rows(engine, plane, scales, lanes=range(LANES)):
-    rows = scales.rearrange("z (q r) c -> r q z c", r=LANES)
-    for r in lanes:
-        engine.dma_start(out=plane[r:P:32, :, :], in_=rows[r].bitcast(I32))
+def load_scale_rows(nc, plane, scales):
+    rows = scales.rearrange("z (q r) c -> r q z c", r=SCALE_ROWS)
+    for r in range(SCALE_ROWS):
+        nc.sync.dma_start(out=plane[r:P:QUADRANT, :, :], in_=rows[r].bitcast(I32))
 
 
 def tile_list_rows_owninput_bygapsize_kernel(
@@ -40,13 +45,13 @@ def tile_list_rows_owninput_bygapsize_kernel(
         keep = ctx.enter_context(tc.tile_pool(name="keep", bufs=1))
         psum = ctx.enter_context(tc.psum_pool(name="psum", bufs=1))
 
-        offsets = keep.tile([P, J // 16], U16, name="offsets")
-        xs_table = keep.tile([P, PASSES, T // 4], I32, name="xs_table", align_bytes=64)
+        offsets = keep.tile([P, J // LIST_ROWS], U16, name="offsets")
+        xs_table = keep.tile([P, PASSES, T // 4], I32, name="xs_table", tag="xs_then_sx", align_bytes=64)
         wa_plane = keep.tile([P, PASSES, N // 4], I32, name="wa_plane", align_bytes=64)
         wb_plane = keep.tile([P, 1, N // 4], I32, name="wb_plane", align_bytes=64)
         ident = keep.tile([P, P], F32, name="ident")
         ones = keep.tile([P, TILES, 1], F32, name="ones")
-        gap = keep.tile([P, TILES, N + 8], F32, name="gap")
+        gap = keep.tile([P, TILES, N + ROW_PAD], F32, name="gap")
 
         nc.vector.memset(xs_table[:, 0, :], 0)
         nc.gpsimd.memset(xs_table[:, 1, :], 0)
@@ -59,29 +64,29 @@ def tile_list_rows_owninput_bygapsize_kernel(
         sx_raw = keep.tile([P, PACK, J], F32, name="sx_raw")
         wa_codes = keep.tile([P, PASSES, N // 2], I32, name="wa_codes", align_bytes=64)
         wb_codes = keep.tile([P, N // 2], I32, name="wb_codes", align_bytes=64)
-        bi_cols = keep.tile([P, 2], F32, name="bi_cols")
-        gm_cols = keep.tile([P, 2], F32, name="gm_cols")
+        bi_cols = keep.tile([P, PAIR], F32, name="bi_cols")
+        gm_cols = keep.tile([P, PAIR], F32, name="gm_cols")
 
         def load_words(z):
             nc.sync.dma_start(out=xw_table[z][:], in_=xt_words[z].rearrange("p c r -> p (c r)").bitcast(I32))
 
         nc.sync.dma_start(out=sx_raw[:], in_=sx.rearrange("(p t) j -> p t j", t=PACK))
         nc.sync.dma_start(offsets[:], offs)
-        load_scale_rows(nc.sync, xs_table, xt_scales)
-        nc.sync.dma_start(out=bi_cols[:], in_=bi.rearrange("o (p c) -> (o p) c", c=2))
+        load_scale_rows(nc, xs_table, xt_scales)
+        nc.sync.dma_start(out=bi_cols[:], in_=bi.rearrange("o (p c) -> (o p) c", c=PAIR))
         load_words(0)
-        nc.sync.dma_start(out=gm_cols[:], in_=gm.rearrange("o (p c) -> (o p) c", c=2))
+        nc.sync.dma_start(out=gm_cols[:], in_=gm.rearrange("o (p c) -> (o p) c", c=PAIR))
         nc.sync.dma_start(out=wb_codes[:], in_=wb_words[0].bitcast(I32))
-        load_scale_rows(nc.sync, wb_plane, wb_scales)
+        load_scale_rows(nc, wb_plane, wb_scales)
         load_words(1)
         nc.sync.dma_start(out=wa_codes[:], in_=wa_words.rearrange("z p c -> p z c").bitcast(I32))
-        load_scale_rows(nc.sync, wa_plane, wa_scales)
+        load_scale_rows(nc, wa_plane, wa_scales)
 
-        def spread(cols, name):
-            bank = psum.tile([P, 2, P], F32, name=name + "_bank")
-            for c in range(2):
-                nc.tensor.transpose(bank[:, c, :], cols[:, c : c + 1].to_broadcast([P, P]), ident[:])
-            rows = keep.tile([P, P, 2], F32, name=name + "_rows")
+        def spread(vector_cols, name):
+            bank = psum.tile([P, PAIR, P], F32, name=name + "_bank")
+            for c in range(PAIR):
+                nc.tensor.transpose(bank[:, c, :], vector_cols[:, c : c + 1].to_broadcast([P, P]), ident[:])
+            rows = keep.tile([P, P, PAIR], F32, name=name + "_rows")
             nc.scalar.copy(out=rows[:], in_=bank[:].rearrange("p c i -> p i c"))
             return rows[:].rearrange("p i c -> p (i c)")
 
@@ -91,25 +96,25 @@ def tile_list_rows_owninput_bygapsize_kernel(
         for z in range(PASSES):
             nc.vector.tensor_copy(out=xs_picked[:, z, :], in_=xs_table[:, z, :].bitcast(U8).indirect(offsets[:]))
 
-        sx_codes = keep.tile([P, J], U32, name="sx_codes", align_bytes=64)
+        sx_codes = keep.tile([P, J], U32, name="sx_codes", tag="xs_then_sx", align_bytes=64)
         sx_plane = keep.tile([P, J], U8, name="sx_plane", align_bytes=64)
         b0 = [psum.tile([P, N], F32, name="b0_%d" % t) for t in range(TILES)]
         for t in range(TILES):
-            cols = slice(t * P, (t + 1) * P)
+            slots = slice(t * P, (t + 1) * P)
             grouped = keep.tile([P, P, PACK], BF16, name="sx_grouped%d" % t, align_bytes=64)
             nc.scalar.copy(
-                out=grouped[:].rearrange("p (c i) r -> p c r i", i=4),
-                in_=sx_raw[:, :, cols].rearrange("p r (c i) -> p c r i", i=4),
+                out=grouped[:].rearrange("p (c i) r -> p c r i", i=LINE),
+                in_=sx_raw[:, :, slots].rearrange("p r (c i) -> p c r i", i=LINE),
             )
             nc.vector.quantize_mx(
-                out=sx_codes[:, cols].bitcast(E5M2X4),
-                scales=sx_plane[:, cols],
+                out=sx_codes[:, slots].bitcast(E5M2X4),
+                scales=sx_plane[:, slots],
                 in_=grouped[:].rearrange("p c r -> p (c r)"),
             )
             nc.tensor.matmul_mx(
                 out=b0[t][:],
-                lhsT=sx_codes[:, cols].bitcast(E5M2X4),
-                lhsT_scale=sx_plane[:, cols],
+                lhsT=sx_codes[:, slots].bitcast(E5M2X4),
+                lhsT_scale=sx_plane[:, slots],
                 rhs=wb_codes[:].bitcast(U8).bitcast(E2M1X4),
                 rhs_scale=wb_plane[:, 0, :].bitcast(U8),
                 start=True,
@@ -119,30 +124,25 @@ def tile_list_rows_owninput_bygapsize_kernel(
         xw_picked = keep.tile([P, PASSES, J], U32, name="xw_picked", align_bytes=64)
         a = [psum.tile([P, N], F32, name="a%d" % t) for t in range(TILES)]
 
-        def a_pass(z, t):
-            cols = slice(t * P, (t + 1) * P)
-            nc.tensor.matmul_mx(
-                out=a[t][:],
-                lhsT=xw_picked[:, z, cols].bitcast(E5M2X4),
-                lhsT_scale=xs_picked[:, z, cols],
-                rhs=wa_codes[:, z, :].bitcast(U8).bitcast(E2M1X4),
-                rhs_scale=wa_plane[:, z, :].bitcast(U8),
-                start=(z == 0),
-                stop=(z == PASSES - 1),
-            )
-
         nc.vector.tensor_copy(out=xw_picked[:, 0, :], in_=xw_table[0][:].bitcast(U32).indirect(offsets[:]))
         b2 = keep.tile([P, TILES, N], F32, name="b2")
         for t in range(TILES):
             nc.vector.tensor_tensor(out=b2[:, t, :], in0=b0[t][:], in1=bi_rows, op=ALU.add)
         gm_rows = spread(gm_cols, "gm")
         for t in range(TILES):
-            nc.vector.tensor_copy(
-                out=xw_picked[:, 1, t * P : (t + 1) * P],
-                in_=xw_table[1][:].bitcast(U32).indirect(offsets[:, t * (P // 16) : (t + 1) * (P // 16)]),
-            )
+            slots = slice(t * P, (t + 1) * P)
+            entries = offsets[:, t * (P // LIST_ROWS) : (t + 1) * (P // LIST_ROWS)]
+            nc.vector.tensor_copy(out=xw_picked[:, 1, slots], in_=xw_table[1][:].bitcast(U32).indirect(entries))
             for z in range(PASSES):
-                a_pass(z, t)
+                nc.tensor.matmul_mx(
+                    out=a[t][:],
+                    lhsT=xw_picked[:, z, slots].bitcast(E5M2X4),
+                    lhsT_scale=xs_picked[:, z, slots],
+                    rhs=wa_codes[:, z, :].bitcast(U8).bitcast(E2M1X4),
+                    rhs_scale=wa_plane[:, z, :].bitcast(U8),
+                    start=(z == 0),
+                    stop=(z == PASSES - 1),
+                )
 
         squares = keep.tile([P, TILES, N + 1], F32, name="squares")
         scaled = keep.tile([P, TILES, N], F32, name="scaled")
@@ -152,12 +152,17 @@ def tile_list_rows_owninput_bygapsize_kernel(
         for t in range(TILES):
             nc.vector.tensor_tensor(out=gap[:, t, 0:N], in0=a[t][:], in1=b2[:, t, :], op=ALU.subtract)
             nc.scalar.activation(
-                out=squares[:, t, :], in_=gap[:, t, 0 : N + 1], func=ACT.Square, scale=1.0 / math.sqrt(N), accum_out=denom[t][:]
+                out=squares[:, t, :],
+                in_=gap[:, t, 0 : N + 1],
+                func=ACT.Square,
+                scale=1.0 / math.sqrt(N),
+                accum_out=denom[t][:],
             )
         for t in range(TILES):
             nc.vector.tensor_tensor(out=scaled[:, t, :], in0=a[t][:], in1=gm_rows, op=ALU.mult)
             nc.vector.reciprocal(out=inverse[t][:], in_=denom[t][:])
-        nc.scalar.activation(out=result[0][:], in_=scaled[:, 0, :], func=ACT.Copy, scale=inverse[0][:])
-        nc.scalar.dma_start(out=out[0:P, :], in_=result[0][:])
-        nc.vector.tensor_scalar(out=result[1][:], in0=scaled[:, 1, :], scalar1=inverse[1][:], scalar2=None, op0=ALU.mult)
-        nc.sync.dma_start(out=out[P : 2 * P, :], in_=result[1][:])
+        for t, queue in enumerate((nc.sync, nc.scalar)):
+            nc.vector.tensor_scalar(
+                out=result[t][:], in0=scaled[:, t, :], scalar1=inverse[t][:], scalar2=None, op0=ALU.mult
+            )
+            queue.dma_start(out=out[t * P : (t + 1) * P, :], in_=result[t][:])

import math
from contextlib import ExitStack

import concourse.mybir as mybir
from concourse.masks import make_identity

K, T, J, N, L = 1024, 1024, 256, 256, 512
FLOPS = 2 * J * N * (K + L)

F32 = mybir.dt.float32
BF16 = mybir.dt.bfloat16
I32 = mybir.dt.int32
U32 = mybir.dt.uint32
U16 = mybir.dt.uint16
U8 = mybir.dt.uint8
E5M2X4 = mybir.dt.float8_e5m2_x4
E2M1X4 = mybir.dt.float4_e2m1fn_x4
ALU = mybir.AluOpType
ACT = mybir.ActivationFunctionType

P = 128
PACK = 4
PASSES = K // (P * PACK)
TILES = J // P
QUADRANT = 32
SCALE_ROWS = 4
LIST_ROWS = 16
LINE = 4
PAIR = N // P
ROW_PAD = 8
EPS = 0.4


def load_scale_rows(nc, plane, scales):
    rows = scales.rearrange("z (q r) c -> r q z c", r=SCALE_ROWS)
    for r in range(SCALE_ROWS):
        nc.sync.dma_start(out=plane[r:P:QUADRANT, :, :], in_=rows[r].bitcast(I32))


def tile_list_rows_owninput_bygapsize_kernel(
    tc, xt_words, xt_scales, wa_words, wa_scales, sx, wb_words, wb_scales, bi, gm, offs, out
):
    nc = tc.nc
    with ExitStack() as ctx:
        keep = ctx.enter_context(tc.tile_pool(name="keep", bufs=1))
        psum = ctx.enter_context(tc.psum_pool(name="psum", bufs=1))

        offsets = keep.tile([P, J // LIST_ROWS], U16, name="offsets")
        xs_table = keep.tile([P, PASSES, T // 4], I32, name="xs_table", tag="xs_then_sx", align_bytes=64)
        wa_plane = keep.tile([P, PASSES, N // 4], I32, name="wa_plane", align_bytes=64)
        wb_plane = keep.tile([P, 1, N // 4], I32, name="wb_plane", align_bytes=64)
        ident = keep.tile([P, P], F32, name="ident")
        ones = keep.tile([P, TILES, 1], F32, name="ones")
        gap = keep.tile([P, TILES, N + ROW_PAD], F32, name="gap")

        nc.vector.memset(xs_table[:, 0, :], 0)
        nc.gpsimd.memset(xs_table[:, 1, :], 0)
        nc.vector.memset(ident[:], 0.0)
        nc.vector.memset(ones[:], 1.0)
        make_identity(nc, ident[:], nomemset=True)
        nc.scalar.activation(out=gap[:, :, N : N + 1], in_=ones[:], func=ACT.Copy, scale=math.sqrt(EPS * N))

        xw_table = [keep.tile([P, T], I32, name="xw_table%d" % z, align_bytes=64) for z in range(PASSES)]
        sx_raw = keep.tile([P, PACK, J], F32, name="sx_raw")
        wa_codes = keep.tile([P, PASSES, N // 2], I32, name="wa_codes", align_bytes=64)
        wb_codes = keep.tile([P, N // 2], I32, name="wb_codes", align_bytes=64)
        bi_cols = keep.tile([P, PAIR], F32, name="bi_cols")
        gm_cols = keep.tile([P, PAIR], F32, name="gm_cols")

        def load_words(z):
            nc.sync.dma_start(out=xw_table[z][:], in_=xt_words[z].rearrange("p c r -> p (c r)").bitcast(I32))

        nc.sync.dma_start(out=sx_raw[:], in_=sx.rearrange("(p t) j -> p t j", t=PACK))
        nc.sync.dma_start(offsets[:], offs)
        load_scale_rows(nc, xs_table, xt_scales)
        nc.sync.dma_start(out=bi_cols[:], in_=bi.rearrange("o (p c) -> (o p) c", c=PAIR))
        load_words(0)
        nc.sync.dma_start(out=gm_cols[:], in_=gm.rearrange("o (p c) -> (o p) c", c=PAIR))
        nc.sync.dma_start(out=wb_codes[:], in_=wb_words[0].bitcast(I32))
        load_scale_rows(nc, wb_plane, wb_scales)
        load_words(1)
        nc.sync.dma_start(out=wa_codes[:], in_=wa_words.rearrange("z p c -> p z c").bitcast(I32))
        load_scale_rows(nc, wa_plane, wa_scales)

        def spread(vector_cols, name):
            bank = psum.tile([P, PAIR, P], F32, name=name + "_bank")
            for c in range(PAIR):
                nc.tensor.transpose(bank[:, c, :], vector_cols[:, c : c + 1].to_broadcast([P, P]), ident[:])
            rows = keep.tile([P, P, PAIR], F32, name=name + "_rows")
            nc.scalar.copy(out=rows[:], in_=bank[:].rearrange("p c i -> p i c"))
            return rows[:].rearrange("p i c -> p (i c)")

        bi_rows = spread(bi_cols, "bi")

        xs_picked = keep.tile([P, PASSES, J], U8, name="xs_picked", align_bytes=64)
        for z in range(PASSES):
            nc.vector.tensor_copy(out=xs_picked[:, z, :], in_=xs_table[:, z, :].bitcast(U8).indirect(offsets[:]))

        sx_codes = keep.tile([P, J], U32, name="sx_codes", tag="xs_then_sx", align_bytes=64)
        sx_plane = keep.tile([P, J], U8, name="sx_plane", align_bytes=64)
        b0 = [psum.tile([P, N], F32, name="b0_%d" % t) for t in range(TILES)]
        for t in range(TILES):
            slots = slice(t * P, (t + 1) * P)
            grouped = keep.tile([P, P, PACK], BF16, name="sx_grouped%d" % t, align_bytes=64)
            nc.scalar.copy(
                out=grouped[:].rearrange("p (c i) r -> p c r i", i=LINE),
                in_=sx_raw[:, :, slots].rearrange("p r (c i) -> p c r i", i=LINE),
            )
            nc.vector.quantize_mx(
                out=sx_codes[:, slots].bitcast(E5M2X4),
                scales=sx_plane[:, slots],
                in_=grouped[:].rearrange("p c r -> p (c r)"),
            )
            nc.tensor.matmul_mx(
                out=b0[t][:],
                lhsT=sx_codes[:, slots].bitcast(E5M2X4),
                lhsT_scale=sx_plane[:, slots],
                rhs=wb_codes[:].bitcast(U8).bitcast(E2M1X4),
                rhs_scale=wb_plane[:, 0, :].bitcast(U8),
                start=True,
                stop=True,
            )

        xw_picked = keep.tile([P, PASSES, J], U32, name="xw_picked", align_bytes=64)
        a = [psum.tile([P, N], F32, name="a%d" % t) for t in range(TILES)]

        nc.vector.tensor_copy(out=xw_picked[:, 0, :], in_=xw_table[0][:].bitcast(U32).indirect(offsets[:]))
        b2 = keep.tile([P, TILES, N], F32, name="b2")
        for t in range(TILES):
            nc.vector.tensor_tensor(out=b2[:, t, :], in0=b0[t][:], in1=bi_rows, op=ALU.add)
        gm_rows = spread(gm_cols, "gm")
        for t in range(TILES):
            slots = slice(t * P, (t + 1) * P)
            entries = offsets[:, t * (P // LIST_ROWS) : (t + 1) * (P // LIST_ROWS)]
            nc.vector.tensor_copy(out=xw_picked[:, 1, slots], in_=xw_table[1][:].bitcast(U32).indirect(entries))
            for z in range(PASSES):
                nc.tensor.matmul_mx(
                    out=a[t][:],
                    lhsT=xw_picked[:, z, slots].bitcast(E5M2X4),
                    lhsT_scale=xs_picked[:, z, slots],
                    rhs=wa_codes[:, z, :].bitcast(U8).bitcast(E2M1X4),
                    rhs_scale=wa_plane[:, z, :].bitcast(U8),
                    start=(z == 0),
                    stop=(z == PASSES - 1),
                )

        squares = keep.tile([P, TILES, N + 1], F32, name="squares")
        scaled = keep.tile([P, TILES, N], F32, name="scaled")
        denom = [keep.tile([P, 1], F32, name="denom%d" % t) for t in range(TILES)]
        inverse = [keep.tile([P, 1], F32, name="inverse%d" % t) for t in range(TILES)]
        result = [keep.tile([P, N], F32, name="result%d" % t) for t in range(TILES)]
        for t in range(TILES):
            nc.vector.tensor_tensor(out=gap[:, t, 0:N], in0=a[t][:], in1=b2[:, t, :], op=ALU.subtract)
            nc.scalar.activation(
                out=squares[:, t, :],
                in_=gap[:, t, 0 : N + 1],
                func=ACT.Square,
                scale=1.0 / math.sqrt(N),
                accum_out=denom[t][:],
            )
        for t in range(TILES):
            nc.vector.tensor_tensor(out=scaled[:, t, :], in0=a[t][:], in1=gm_rows, op=ALU.mult)
            nc.vector.reciprocal(out=inverse[t][:], in_=denom[t][:])
        for t, queue in enumerate((nc.sync, nc.scalar)):
            nc.vector.tensor_scalar(
                out=result[t][:], in0=scaled[:, t, :], scalar1=inverse[t][:], scalar2=None, op0=ALU.mult
            )
            queue.dma_start(out=out[t * P : (t + 1) * P, :], in_=result[t][:])
